import numpy as np
import ml_dtypes


def mxq(x, axis, fmt="e4m3"):
    dtype, down = {"e4m3": (ml_dtypes.float8_e4m3fn, 7), "e5m2": (ml_dtypes.float8_e5m2, 14)}[fmt]
    v = np.moveaxis(np.asarray(x, np.float32).astype(ml_dtypes.bfloat16).astype(np.float64), axis, -1)
    blocks = v.reshape(v.shape[:-1] + (-1, 32))
    amax = np.abs(blocks).max(-1, keepdims=True)
    byte = np.maximum(np.where(amax > 0, np.frexp(amax)[1] - 1 + 127, 0) - down, 1)
    scale = np.exp2(byte - 127.0)
    codes = (blocks / scale).astype(np.float32).astype(dtype).astype(np.float64)
    return np.moveaxis((codes * scale).reshape(v.shape), -1, axis)


WIDE = False


def mx_kscale(k):
    if not WIDE:
        return np.ones(k)
    levels = np.array([10, -10, 5, -5, 0])
    if k % 512:
        return np.exp2(np.random.permutation(np.resize(levels, k // 32))).repeat(32)
    a = np.empty((k // 512, 16))
    for p in range(k // 512):
        a[p, :8] = np.random.permutation(np.resize(levels, 8))
        for g in range(8):
            far = levels[np.abs(levels - a[p, g]) >= 10]
            a[p, g + 8] = far[np.random.randint(len(far))]
    return np.exp2(a.ravel()).repeat(32)


def f64(x):
    return np.asarray(x).astype(np.float64)


def striped(idx):
    return np.tile(idx.reshape(-1, 16).T, (8, 1)).astype(np.uint16)


def unstriped(offs):
    return offs[:16].T.reshape(-1).astype(np.int64)


E2M1 = np.array([0.0, 0.5, 1.0, 1.5, 2.0, 3.0, 4.0, 6.0, -0.0, -0.5, -1.0, -1.5, -2.0, -3.0, -4.0, -6.0])


def pack_weight(w, fmt):
    k, n = w.shape
    w = f64(np.asarray(w, np.float32).astype(ml_dtypes.bfloat16)).reshape(k // 32, 32, n)
    amax = np.abs(w).max(1)
    if fmt == "e4m3":
        byte = np.frexp(amax)[1] - 1 + 127 - 7
    else:
        mant, ex = np.frexp(amax / 6.0)
        byte = np.where(mant > 0.5, ex, ex - 1) + 127
    byte = np.clip(np.where(amax > 0, byte, 1), 1, 254)
    scaled = (w * np.exp2(127.0 - byte)[:, None, :]).reshape(k, n).astype(np.float32)
    by_word = np.ascontiguousarray(scaled.reshape(k // 512, 128, 4, n).transpose(0, 1, 3, 2))
    if fmt == "e4m3":
        words = by_word.astype(ml_dtypes.float8_e4m3fn).view(np.uint8)
    else:
        c = by_word.astype(ml_dtypes.float4_e2m1fn).view(np.uint8) & 0xF
        words = (c[..., 0::2] | (c[..., 1::2] << 4)).reshape(k // 512, 128, 2 * n)
    return np.ascontiguousarray(words), np.ascontiguousarray(byte.astype(np.uint8).reshape(k // 512, 16, n))


def unpack_weight(words, scales, fmt):
    g, _, n = scales.shape
    words = np.ascontiguousarray(words).reshape(g, 128, n, -1)
    if fmt == "e4m3":
        vals = words.view(ml_dtypes.float8_e4m3fn).astype(np.float64)
    else:
        nib = np.empty((g, 128, n, 4), np.uint8)
        nib[..., 0::2] = words & 0xF
        nib[..., 1::2] = words >> 4
        vals = E2M1[nib]
    vals = vals * np.repeat(np.exp2(scales.astype(np.float64) - 127.0), 8, axis=1)[..., None]
    return vals.transpose(0, 1, 3, 2).reshape(g * 512, n)


def gelu(v):
    return 0.5 * v * (1.0 + np.tanh(np.sqrt(2.0 / np.pi) * (v + 0.044715 * v**3)))


K, T, E, C, H, N = 1536, 1536, 6, 256, 512, 512


def by_expert(wq, xq):
    return np.concatenate([wq[e].T @ xq[:, e * C:(e + 1) * C] for e in range(E)], axis=1)


def setup_inputs():
    n = np.random.standard_normal
    s = mx_kscale(K)[:, None]
    u = mx_kscale(H)
    w1 = [pack_weight(m, "e2m1") for m in n((E, K, H)) / np.sqrt(K) / s[None] * u[None, None, :]]
    w2 = [pack_weight(m, "e2m1") for m in n((E, H, N)) / np.sqrt(H) / u[None, :, None]]
    x = pack_weight(n((K, T)) * s, "e4m3")
    return {
        "x_words": x[0],
        "x_scales": x[1],
        "w1_words": np.stack([m[0] for m in w1]),
        "w1_scales": np.stack([m[1] for m in w1]),
        "w2_words": np.stack([m[0] for m in w2]),
        "w2_scales": np.stack([m[1] for m in w2]),
        "gate": np.tile(np.random.uniform(0.2, 1.0, E * C), (N, 1)).astype(np.float32),
        "offs": striped(np.random.permutation(T)[:E * C]),
    }


def reference(x_words, x_scales, w1_words, w1_scales, w2_words, w2_scales, gate, offs):
    idx = unstriped(offs)
    w1 = np.stack([unpack_weight(w1_words[e], w1_scales[e], "e2m1") for e in range(E)])
    w2 = np.stack([unpack_weight(w2_words[e], w2_scales[e], "e2m1") for e in range(E)])
    xq = unpack_weight(x_words, x_scales, "e4m3")[:, idx]
    h = gelu(by_expert(w1, xq))
    y = by_expert(w2, mxq(h, 0, "e4m3"))
    out = np.zeros((N, T))
    out[:, idx] = f64(gate) * y
    return out

@@ -1,0 +1,198 @@
+from contextlib import ExitStack
+
+import concourse.mybir as mybir
+from concourse.masks import make_identity
+
+K, T, E, C, H, N = 1536, 1536, 6, 256, 512, 512
+P = 128
+PASSES = K // 512
+F32 = mybir.dt.float32
+BF16 = mybir.dt.bfloat16
+I32 = mybir.dt.int32
+U32 = mybir.dt.uint32
+U16 = mybir.dt.uint16
+U8 = mybir.dt.uint8
+FP8X4 = mybir.dt.float8_e4m3fn_x4
+FP4X4 = mybir.dt.float4_e2m1fn_x4
+GELU = mybir.ActivationFunctionType.Gelu_apprx_tanh
+MULT = mybir.AluOpType.mult
+
+FLOPS = 2 * E * C * (K * H + H * N)
+BYTES = K * T + K * T // 32 + E * (K * H + H * N) // 2 + E * (K * H + H * N) // 32 + 4 * E * C + 4 * N * T + 2 * P * (E * C // 16)
+
+
+def tile_moe_pkd_mlp_gelu_kernel(
+    tc, x_words, x_scales, w1_words, w1_scales, w2_words, w2_scales, gate, offs, out
+):
+    nc = tc.nc
+    with ExitStack() as ctx:
+        keep = ctx.enter_context(tc.tile_pool(name="keep", bufs=1))
+        reuse = ctx.enter_context(tc.tile_pool(name="reuse", bufs=1))
+        ring = ctx.enter_context(tc.tile_pool(name="ring", bufs=3))
+        psum = ctx.enter_context(tc.psum_pool(name="psum", bufs=1))
+
+        offsets = keep.tile([P, E * C // 16], U16, name="offsets")
+        nc.sync.dma_start(offsets[:], offs)
+
+        def slots_of(e0, e1):
+            return offsets[:, e0 * C // 16 : e1 * C // 16]
+
+        xs_raw = keep.tile([P, T], U8, name="xs_raw", align_bytes=64)
+        xs_rows = x_scales.rearrange("a (h c r) t -> c (a h) r t", h=2, c=2).bitcast(I32)
+        xs_raw32 = xs_raw[:].bitcast(I32)
+        for c in range(2):
+            base = 8 + 32 * c
+            nc.sync.dma_start(out=xs_raw32[base : base + 16, :], in_=xs_rows[c, 0:4])
+            nc.sync.dma_start(out=xs_raw32[base + 16 : base + 24, :], in_=xs_rows[c, 4:6])
+
+        xw_first = reuse.tile([P, T], I32, name="xw_first", align_bytes=64, offset=2 * T)
+        nc.sync.dma_start(out=xw_first[:], in_=x_words[0].rearrange("p t r -> p (t r)").bitcast(I32))
+        xw_rest = keep.tile([P, PASSES - 1, T], I32, name="xw_rest", align_bytes=64)
+        nc.sync.dma_start(out=xw_rest[:], in_=x_words[1:PASSES].rearrange("a p t r -> p a (t r)").bitcast(I32))
+
+        def load_planes(planes, scales, e0, e1, queues):
+            n_planes = (e1 - e0) * scales.shape[1]
+            rows = scales[e0:e1].rearrange("e s (q r) n -> r q (e s) n", r=4).bitcast(I32)
+            for r in range(4):
+                queues[r].dma_start(out=planes[:].bitcast(I32)[r:P:32, 0:n_planes, :], in_=rows[r])
+
+        w1w = {}
+
+        def load_w1(e0, e1, tag):
+            words = keep.tile([P, (e1 - e0) * PASSES, 2 * H], U8, name=f"w1_words{e0}", tag=tag, align_bytes=64)
+            nc.sync.dma_start(
+                out=words[:].bitcast(I32), in_=w1_words[e0:e1].rearrange("e s p b -> p (e s) b").bitcast(I32)
+            )
+            for e in range(e0, e1):
+                w1w[e] = (words, (e - e0) * PASSES)
+
+        load_w1(0, 1, "w1_first")
+        w1s = keep.tile([P, 4 * PASSES, H], U8, name="w1_planes", align_bytes=64)
+        nc.vector.memset(w1s[:].bitcast(I32), 0)
+        load_planes(w1s, w1_scales, 0, 4, [nc.scalar] * 4)
+        for lo, hi in ((0, 8), (32, 40), (64, 128)):
+            nc.vector.memset(xs_raw32[lo:hi, :], 0)
+        w2s = keep.tile([P, E, N], U8, name="w2_planes", align_bytes=64)
+        nc.vector.memset(w2s[:].bitcast(I32), 0)
+        load_planes(w2s, w2_scales, 0, E, [nc.scalar, nc.scalar, nc.sync, nc.sync])
+
+        ident = keep.tile([P, P], F32, name="ident")
+        make_identity(nc, ident[:])
+
+        xs_slots = keep.tile([P, E * C], U8, name="xs_slots", tag="xs_slots", align_bytes=64)
+        for e0, e1 in ((0, 3), (3, 6)):
+            nc.vector.tensor_copy(xs_slots[:, e0 * C : e1 * C], xs_raw[:].indirect(slots_of(e0, e1)))
+        xs_slots32 = xs_slots[:].bitcast(I32)
+        x_planes = []
+        for a in range(PASSES):
+            plane = keep.tile([P, E * C], U8, name=f"x_plane{a}", align_bytes=64)
+            for h in range(2):
+                src = 8 + 4 * (2 * a + h)
+                nc.scalar.dma_start(out=plane[:].bitcast(I32)[64 * h : 64 * h + 64, :], in_=xs_slots32[src : src + 64, :])
+            x_planes.append(plane)
+        load_w1(1, 3, "xs_slots")
+
+        gathered = {}
+
+        def gather_words(a, e0, e1, tag):
+            window = xw_first[:] if a == 0 else xw_rest[:, a - 1, :]
+            words = keep.tile([P, (e1 - e0) * C], U32, name=f"xg{a}_{e0}", tag=tag, align_bytes=64)
+            nc.vector.tensor_copy(words[:], window.bitcast(U32).indirect(slots_of(e0, e1)))
+            for e in range(e0, e1):
+                gathered[a, e] = (words, (e - e0) * C)
+
+        gather_words(0, 0, 3, "xg0_0")
+        gather_words(0, 3, 6, "xg0_3")
+        w2w = reuse.tile([P, E, 2 * N], U8, name="w2_words_sb", align_bytes=64, offset=0)
+        nc.sync.dma_start(out=w2w[:].bitcast(I32), in_=w2_words.rearrange("e s p b -> p (e s) b").bitcast(I32))
+        gate_sb = reuse.tile([P, E * C], F32, name="gate_sb", align_bytes=64, offset=4 * T)
+        nc.sync.dma_start(out=gate_sb[:], in_=gate[0:P, :])
+        for e in range(3):
+            gather_words(1, e, e + 1, f"xg1_{e}")
+            gather_words(2, e, e + 1, f"xg2_{e}")
+        gather_words(1, 3, 6, "xg1_3")
+        gather_words(2, 3, 4, "xg2_3")
+
+        y_sb = [keep.tile([P, 2, E * C], F32, name=f"y_sb{j}") for j in range(2)]
+
+        def first_layer(e):
+            w1_tile, w1_at = w1w[e]
+            turned = psum.tile([P, 2, 2, P], F32, name="turned", tag=f"turned{e % 2}")
+            h_cols = keep.tile([P, 4 * C], BF16, name=f"h_cols{e}", tag=f"h_cols{e}", align_bytes=64)
+            for half in range(2):
+                acc = psum.tile([P, H], F32, name="acc", tag=f"acc{(2 * e + half) % 4}")
+                for a in range(PASSES):
+                    words, at = gathered[a, e]
+                    col = e * C + half * P
+                    nc.tensor.matmul_mx(
+                        out=acc[:],
+                        lhsT=words[:, at + half * P : at + (half + 1) * P].bitcast(FP8X4),
+                        lhsT_scale=x_planes[a][:, col : col + P],
+                        rhs=w1_tile[:, w1_at + a, :].bitcast(FP4X4),
+                        rhs_scale=w1s[:, (e % 4) * PASSES + a, :],
+                        start=(a == 0),
+                        stop=(a == PASSES - 1),
+                    )
+                h_rows = ring.tile([P, H], BF16, name="h_rows", align_bytes=64)
+                nc.scalar.activation(
+                    out=h_rows[:].rearrange("s (u p d) -> s u p d", u=2, d=2),
+                    in_=acc[:].rearrange("s (p u d) -> s u p d", u=2, d=2),
+                    func=GELU,
+                )
+                pairs = h_rows[:].bitcast(F32)
+                for u in range(2):
+                    nc.tensor.transpose(turned[:, half, u, :], pairs[:, u * P : (u + 1) * P], ident[:])
+                nc.scalar.copy(
+                    out=h_cols[:].bitcast(F32)[:, half * C : (half + 1) * C].rearrange("p (s u) -> p s u", u=2),
+                    in_=turned[:, half].rearrange("p u s -> p s u"),
+                )
+            codes = keep.tile([P, C], U32, name=f"h_codes{e}", tag=f"h_codes{e}", align_bytes=64)
+            scales = keep.tile([P, C], U8, name=f"h_scales{e}", align_bytes=64)
+            nc.vector.quantize_mx(out=codes[:].bitcast(FP8X4), scales=scales[:], in_=h_cols[:])
+            return codes, scales
+
+        def second_layer(e, codes, scales):
+            for j in range(2):
+                bank = f"y{j}" if e < 3 else ("turned1", "acc3")[j]
+                acc = psum.tile([P, 2, C], F32, name="y_acc", tag=bank)
+                for b in range(2):
+                    nb = 2 * j + b
+                    nc.tensor.matmul_mx(
+                        out=acc[:, b, :],
+                        lhsT=w2w[:, e, 2 * P * nb : 2 * P * (nb + 1)].bitcast(FP4X4),
+                        lhsT_scale=w2s[:, e, P * nb : P * (nb + 1)],
+                        rhs=codes[:].bitcast(FP8X4),
+                        rhs_scale=scales[:],
+                        start=True,
+                        stop=True,
+                    )
+                nc.scalar.copy(out=y_sb[j][:, :, e * C : (e + 1) * C], in_=acc[:])
+
+        windows = {}
+
+        def scatter(nb, e0, e1, tag=None):
+            if nb not in windows:
+                windows[nb] = keep.tile([P, T], F32, name=f"window{nb}", tag=tag, align_bytes=64)
+            cols = slice(e0 * C, e1 * C)
+            nc.vector.tensor_tensor(
+                windows[nb][:].indirect(slots_of(e0, e1)), y_sb[nb // 2][:, nb % 2, cols], gate_sb[:, cols], MULT
+            )
+
+        second_layer(0, *first_layer(0))
+        load_w1(3, E, "w1_first")
+        gather_words(2, 4, 6, "h_cols0")
+        scatter(0, 0, 1, "window0")
+        second_layer(1, *first_layer(1))
+        load_planes(w1s, w1_scales, 4, E, [nc.sync] * 4)
+        second_layer(2, *first_layer(2))
+        scatter(1, 0, 1, "h_cols2")
+        scatter(2, 0, 1, "h_codes2")
+        for nb in range(3):
+            scatter(nb, 1, 3)
+        hidden = [first_layer(e) for e in range(3, E)]
+        for e in range(3, E):
+            second_layer(e, *hidden[e - 3])
+        scatter(3, 0, 3, "h_cols5")
+        for nb in range(4):
+            scatter(nb, 3, E)
+            nc.sync.dma_start(out=out[nb * P : (nb + 1) * P, :], in_=windows[nb][:])

@@ -6,6 +6,9 @@ from concourse.masks import make_identity
 K, T, E, C, H, N = 1536, 1536, 6, 256, 512, 512
 P = 128
 PASSES = K // 512
+BLOCKS = N // P
+EARLY = E // 2
+MARGIN = 64
 F32 = mybir.dt.float32
 BF16 = mybir.dt.bfloat16
 I32 = mybir.dt.int32
@@ -18,7 +21,8 @@ GELU = mybir.ActivationFunctionType.Gelu_apprx_tanh
 MULT = mybir.AluOpType.mult
 
 FLOPS = 2 * E * C * (K * H + H * N)
-BYTES = K * T + K * T // 32 + E * (K * H + H * N) // 2 + E * (K * H + H * N) // 32 + 4 * E * C + 4 * N * T + 2 * P * (E * C // 16)
+WEIGHTS = E * (K * H + H * N)
+BYTES = K * T + K * T // 32 + WEIGHTS // 2 + WEIGHTS // 32 + 4 * E * C + 4 * N * T + 2 * P * (E * C // 16)
 
 
 def tile_moe_pkd_mlp_gelu_kernel(
@@ -27,7 +31,8 @@ def tile_moe_pkd_mlp_gelu_kernel(
     nc = tc.nc
     with ExitStack() as ctx:
         keep = ctx.enter_context(tc.tile_pool(name="keep", bufs=1))
-        reuse = ctx.enter_context(tc.tile_pool(name="reuse", bufs=1))
+        at_scales = ctx.enter_context(tc.tile_pool(name="at_scales", bufs=1))
+        at_words = ctx.enter_context(tc.tile_pool(name="at_words", bufs=1))
         ring = ctx.enter_context(tc.tile_pool(name="ring", bufs=3))
         psum = ctx.enter_context(tc.psum_pool(name="psum", bufs=1))
 
@@ -37,103 +42,144 @@ def tile_moe_pkd_mlp_gelu_kernel(
         def slots_of(e0, e1):
             return offsets[:, e0 * C // 16 : e1 * C // 16]
 
-        xs_raw = keep.tile([P, T], U8, name="xs_raw", align_bytes=64)
+        early_rows = (EARLY - 1) * PASSES + EARLY
+        last_rows = (E - EARLY) * (PASSES + 1)
+        last_bytes = last_rows * 2 * H
+        early_bytes = early_rows * 2 * H
+
+        xs_tile = at_scales.tile([P, T + 2 * MARGIN], U8, name="xs_tile", align_bytes=64, offset=early_bytes - MARGIN)
+        xs_tokens = xs_tile[:, MARGIN : MARGIN + T]
         xs_rows = x_scales.rearrange("a (h c r) t -> c (a h) r t", h=2, c=2).bitcast(I32)
-        xs_raw32 = xs_raw[:].bitcast(I32)
+        xs_tokens32 = xs_tokens.bitcast(I32)
         for c in range(2):
             base = 8 + 32 * c
-            nc.sync.dma_start(out=xs_raw32[base : base + 16, :], in_=xs_rows[c, 0:4])
-            nc.sync.dma_start(out=xs_raw32[base + 16 : base + 24, :], in_=xs_rows[c, 4:6])
+            nc.sync.dma_start(out=xs_tokens32[base : base + 16, :], in_=xs_rows[c, 0:4])
+            nc.sync.dma_start(out=xs_tokens32[base + 16 : base + 24, :], in_=xs_rows[c, 4:6])
 
-        xw_first = reuse.tile([P, T], I32, name="xw_first", align_bytes=64, offset=2 * T)
-        nc.sync.dma_start(out=xw_first[:], in_=x_words[0].rearrange("p t r -> p (t r)").bitcast(I32))
-        xw_rest = keep.tile([P, PASSES - 1, T], I32, name="xw_rest", align_bytes=64)
-        nc.sync.dma_start(out=xw_rest[:], in_=x_words[1:PASSES].rearrange("a p t r -> p a (t r)").bitcast(I32))
+        xw_tile = at_words.tile([P, T + MARGIN // 2], I32, name="xw_tile", align_bytes=64, offset=last_bytes - MARGIN)
+        xw_first = xw_tile[:, MARGIN // 4 : MARGIN // 4 + T]
+        nc.sync.dma_start(out=xw_first, in_=x_words[0].rearrange("p t r -> p (t r)").bitcast(I32))
 
-        def load_planes(planes, scales, e0, e1, queues):
+        def load_planes(planes, at, scales, e0, e1):
             n_planes = (e1 - e0) * scales.shape[1]
             rows = scales[e0:e1].rearrange("e s (q r) n -> r q (e s) n", r=4).bitcast(I32)
             for r in range(4):
-                queues[r].dma_start(out=planes[:].bitcast(I32)[r:P:32, 0:n_planes, :], in_=rows[r])
+                nc.sync.dma_start(out=planes[:].bitcast(I32)[r:P:32, at : at + n_planes, :], in_=rows[r])
 
-        w1w = {}
+        w1_codes = {}
+        w1_planes = {}
 
-        def load_w1(e0, e1, tag):
-            words = keep.tile([P, (e1 - e0) * PASSES, 2 * H], U8, name=f"w1_words{e0}", tag=tag, align_bytes=64)
+        def load_w1(words, at, e0, e1):
             nc.sync.dma_start(
-                out=words[:].bitcast(I32), in_=w1_words[e0:e1].rearrange("e s p b -> p (e s) b").bitcast(I32)
+                out=words[:, at : at + (e1 - e0) * PASSES, :].bitcast(I32),
+                in_=w1_words[e0:e1].rearrange("e s p b -> p (e s) b").bitcast(I32),
             )
             for e in range(e0, e1):
-                w1w[e] = (words, (e - e0) * PASSES)
+                w1_codes[e] = words[:, at + (e - e0) * PASSES : at + (e - e0 + 1) * PASSES, :]
 
-        load_w1(0, 1, "w1_first")
-        w1s = keep.tile([P, 4 * PASSES, H], U8, name="w1_planes", align_bytes=64)
-        nc.vector.memset(w1s[:].bitcast(I32), 0)
-        load_planes(w1s, w1_scales, 0, 4, [nc.scalar] * 4)
-        for lo, hi in ((0, 8), (32, 40), (64, 128)):
-            nc.vector.memset(xs_raw32[lo:hi, :], 0)
-        w2s = keep.tile([P, E, N], U8, name="w2_planes", align_bytes=64)
-        nc.vector.memset(w2s[:].bitcast(I32), 0)
-        load_planes(w2s, w2_scales, 0, E, [nc.scalar, nc.scalar, nc.sync, nc.sync])
+        def name_w1_planes(planes, e0, e1):
+            for e in range(e0, e1):
+                w1_planes[e] = planes[:, (e - e0) * PASSES : (e - e0 + 1) * PASSES, :]
+
+        first_words = keep.tile([P, PASSES, 2 * H], U8, name="first_words", tag="first_words", align_bytes=64)
+        load_w1(first_words, 0, 0, 1)
+        first_planes = keep.tile([P, PASSES, H], U8, name="first_planes", align_bytes=64)
+        nc.gpsimd.memset(first_planes[:].bitcast(I32), 0)
+        load_planes(first_planes, 0, w1_scales, 0, 1)
+        name_w1_planes(first_planes, 0, 1)
+        xw_rest = keep.tile([P, PASSES - 1, T], I32, name="xw_rest", align_bytes=64)
+        nc.sync.dma_start(out=xw_rest[:], in_=x_words[1:PASSES].rearrange("a p t r -> p a (t r)").bitcast(I32))
+        for lo, hi in ((0, 8), (32, 40), (64, P)):
+            nc.vector.memset(xs_tokens32[lo:hi, :], 0)
 
         ident = keep.tile([P, P], F32, name="ident")
         make_identity(nc, ident[:])
 
-        xs_slots = keep.tile([P, E * C], U8, name="xs_slots", tag="xs_slots", align_bytes=64)
-        for e0, e1 in ((0, 3), (3, 6)):
-            nc.vector.tensor_copy(xs_slots[:, e0 * C : e1 * C], xs_raw[:].indirect(slots_of(e0, e1)))
-        xs_slots32 = xs_slots[:].bitcast(I32)
-        x_planes = []
-        for a in range(PASSES):
-            plane = keep.tile([P, E * C], U8, name=f"x_plane{a}", align_bytes=64)
-            for h in range(2):
-                src = 8 + 4 * (2 * a + h)
-                nc.scalar.dma_start(out=plane[:].bitcast(I32)[64 * h : 64 * h + 64, :], in_=xs_slots32[src : src + 64, :])
-            x_planes.append(plane)
-        load_w1(1, 3, "xs_slots")
+        xs_slots = keep.tile([P, E * C], U8, name="xs_slots", align_bytes=64)
+        for e0, e1 in ((0, EARLY), (EARLY, E)):
+            nc.vector.tensor_copy(xs_slots[:, e0 * C : e1 * C], xs_tokens.indirect(slots_of(e0, e1)))
 
-        gathered = {}
+        x_planes = {}
+
+        def move_scale_rows(planes, e0, e1, queue):
+            cols = slice(e0 * C // 4, e1 * C // 4)
+            for a in range(PASSES):
+                for h in range(2):
+                    src = 8 + 4 * (2 * a + h)
+                    queue.dma_start(
+                        out=planes[:].bitcast(I32)[64 * h : 64 * h + 64, a, :],
+                        in_=xs_slots[:].bitcast(I32)[src : src + 64, cols],
+                    )
+            for e in range(e0, e1):
+                x_planes[e] = planes[:, :, (e - e0) * C : (e - e0 + 1) * C]
+
+        early_x_planes = keep.tile([P, PASSES, EARLY * C], U8, name="early_x_planes", align_bytes=64)
+        move_scale_rows(early_x_planes, 0, EARLY, nc.scalar)
+        second_planes = at_scales.tile([P, PASSES, H], U8, name="second_planes", align_bytes=64, offset=early_bytes)
+        load_planes(second_planes, 0, w1_scales, 1, 2)
+        name_w1_planes(second_planes, 1, 2)
+
+        x_codes = {}
 
         def gather_words(a, e0, e1, tag):
-            window = xw_first[:] if a == 0 else xw_rest[:, a - 1, :]
-            words = keep.tile([P, (e1 - e0) * C], U32, name=f"xg{a}_{e0}", tag=tag, align_bytes=64)
+            window = xw_first if a == 0 else xw_rest[:, a - 1, :]
+            words = keep.tile([P, (e1 - e0) * C], U32, name=f"x_codes{a}_{e0}", tag=tag, align_bytes=64)
             nc.vector.tensor_copy(words[:], window.bitcast(U32).indirect(slots_of(e0, e1)))
             for e in range(e0, e1):
-                gathered[a, e] = (words, (e - e0) * C)
+                x_codes[a, e] = words[:, (e - e0) * C : (e - e0 + 1) * C]
 
-        gather_words(0, 0, 3, "xg0_0")
-        gather_words(0, 3, 6, "xg0_3")
-        w2w = reuse.tile([P, E, 2 * N], U8, name="w2_words_sb", align_bytes=64, offset=0)
-        nc.sync.dma_start(out=w2w[:].bitcast(I32), in_=w2_words.rearrange("e s p b -> p (e s) b").bitcast(I32))
-        gate_sb = reuse.tile([P, E * C], F32, name="gate_sb", align_bytes=64, offset=4 * T)
+        gather_words(0, 0, EARLY, "x_codes0_early")
+        gather_words(0, EARLY, E, "x_codes0_last")
+
+        early_words = at_scales.tile([P, early_rows, 2 * H], U8, name="early_words", align_bytes=64, offset=0)
+        gate_sb = at_scales.tile([P, E * C], F32, name="gate_sb", align_bytes=64, offset=early_bytes + T)
+        last_words = at_words.tile([P, last_rows, 2 * H], U8, name="last_words", align_bytes=64, offset=0)
+        mid_planes = at_words.tile([P, 2 * PASSES + E, H], U8, name="mid_planes", align_bytes=64, offset=last_bytes)
+        last_x_planes = at_words.tile(
+            [P, PASSES, (E - EARLY) * C], U8, name="last_x_planes", align_bytes=64, offset=last_bytes + 4 * T
+        )
+        w2_codes = [early_words[:, (EARLY - 1) * PASSES :, :], last_words[:, (E - EARLY) * PASSES :, :]]
+        w2_rows = w2_words.rearrange("e s p b -> p (e s) b").bitcast(I32)
+        load_w1(early_words, 0, 1, 2)
+        nc.sync.dma_start(out=w2_codes[0].bitcast(I32), in_=w2_rows[:, 0:EARLY, :])
         nc.sync.dma_start(out=gate_sb[:], in_=gate[0:P, :])
-        for e in range(3):
-            gather_words(1, e, e + 1, f"xg1_{e}")
-            gather_words(2, e, e + 1, f"xg2_{e}")
-        gather_words(1, 3, 6, "xg1_3")
-        gather_words(2, 3, 4, "xg2_3")
+        load_w1(early_words, PASSES, 2, EARLY)
+        load_planes(mid_planes, 2 * PASSES, w2_scales, 0, E)
+        load_planes(mid_planes, 0, w1_scales, 2, 4)
+        move_scale_rows(last_x_planes, EARLY, E, nc.sync)
+        load_w1(last_words, 0, EARLY, E)
+        nc.sync.dma_start(out=w2_codes[1].bitcast(I32), in_=w2_rows[:, EARLY:E, :])
+        name_w1_planes(mid_planes, 2, 4)
+        w2_planes = mid_planes[:, 2 * PASSES :, :]
 
-        y_sb = [keep.tile([P, 2, E * C], F32, name=f"y_sb{j}") for j in range(2)]
+        for e in range(EARLY):
+            gather_words(1, e, e + 1, f"x_codes1_{e}")
+            gather_words(2, e, e + 1, f"x_codes2_{e}")
+        gather_words(1, EARLY, E, "x_codes1_last")
+        gather_words(2, 3, 4, "x_codes2_3")
 
-        def first_layer(e):
-            w1_tile, w1_at = w1w[e]
+        y_sb = [keep.tile([P, 2, E * C], F32, name=f"y_sb{j}") for j in range(BLOCKS // 2)]
+
+        def first_layer(e, banks, row_tags=None, copy_by_half=False):
             turned = psum.tile([P, 2, 2, P], F32, name="turned", tag=f"turned{e % 2}")
             h_cols = keep.tile([P, 4 * C], BF16, name=f"h_cols{e}", tag=f"h_cols{e}", align_bytes=64)
             for half in range(2):
-                acc = psum.tile([P, H], F32, name="acc", tag=f"acc{(2 * e + half) % 4}")
+                slots = slice(half * P, (half + 1) * P)
+                acc = psum.tile([P, H], F32, name="acc", tag=banks[half])
                 for a in range(PASSES):
-                    words, at = gathered[a, e]
-                    col = e * C + half * P
                     nc.tensor.matmul_mx(
                         out=acc[:],
-                        lhsT=words[:, at + half * P : at + (half + 1) * P].bitcast(FP8X4),
-                        lhsT_scale=x_planes[a][:, col : col + P],
-                        rhs=w1_tile[:, w1_at + a, :].bitcast(FP4X4),
-                        rhs_scale=w1s[:, (e % 4) * PASSES + a, :],
+                        lhsT=x_codes[a, e][:, slots].bitcast(FP8X4),
+                        lhsT_scale=x_planes[e][:, a, slots],
+                        rhs=w1_codes[e][:, a, :].bitcast(FP4X4),
+                        rhs_scale=w1_planes[e][:, a, :],
                         start=(a == 0),
                         stop=(a == PASSES - 1),
                     )
-                h_rows = ring.tile([P, H], BF16, name="h_rows", align_bytes=64)
+                if row_tags is None:
+                    h_rows = ring.tile([P, H], BF16, name="h_rows", align_bytes=64)
+                else:
+                    h_rows = keep.tile([P, H], BF16, name="h_rows_last", tag=row_tags[half], align_bytes=64)
                 nc.scalar.activation(
                     out=h_rows[:].rearrange("s (u p d) -> s u p d", u=2, d=2),
                     in_=acc[:].rearrange("s (p u d) -> s u p d", u=2, d=2),
@@ -142,31 +188,39 @@ def tile_moe_pkd_mlp_gelu_kernel(
                 pairs = h_rows[:].bitcast(F32)
                 for u in range(2):
                     nc.tensor.transpose(turned[:, half, u, :], pairs[:, u * P : (u + 1) * P], ident[:])
+                if copy_by_half:
+                    nc.scalar.copy(
+                        out=h_cols[:].bitcast(F32)[:, half * C : (half + 1) * C].rearrange("p (s u) -> p s u", u=2),
+                        in_=turned[:, half].rearrange("p u s -> p s u"),
+                    )
+            if not copy_by_half:
                 nc.scalar.copy(
-                    out=h_cols[:].bitcast(F32)[:, half * C : (half + 1) * C].rearrange("p (s u) -> p s u", u=2),
-                    in_=turned[:, half].rearrange("p u s -> p s u"),
+                    out=h_cols[:].bitcast(F32).rearrange("p (h s u) -> p h s u", h=2, u=2),
+                    in_=turned[:].rearrange("p h u s -> p h s u"),
                 )
+            return h_cols
+
+        def quantize(e, h_cols):
             codes = keep.tile([P, C], U32, name=f"h_codes{e}", tag=f"h_codes{e}", align_bytes=64)
             scales = keep.tile([P, C], U8, name=f"h_scales{e}", align_bytes=64)
             nc.vector.quantize_mx(out=codes[:].bitcast(FP8X4), scales=scales[:], in_=h_cols[:])
             return codes, scales
 
-        def second_layer(e, codes, scales):
-            for j in range(2):
-                bank = f"y{j}" if e < 3 else ("turned1", "acc3")[j]
-                acc = psum.tile([P, 2, C], F32, name="y_acc", tag=bank)
-                for b in range(2):
-                    nb = 2 * j + b
-                    nc.tensor.matmul_mx(
-                        out=acc[:, b, :],
-                        lhsT=w2w[:, e, 2 * P * nb : 2 * P * (nb + 1)].bitcast(FP4X4),
-                        lhsT_scale=w2s[:, e, P * nb : P * (nb + 1)],
-                        rhs=codes[:].bitcast(FP8X4),
-                        rhs_scale=scales[:],
-                        start=True,
-                        stop=True,
-                    )
-                nc.scalar.copy(out=y_sb[j][:, :, e * C : (e + 1) * C], in_=acc[:])
+        def second_layer(e, j, quantized, bank):
+            codes, scales = quantized
+            acc = psum.tile([P, 2, C], F32, name="y_acc", tag=bank)
+            for b in range(2):
+                nb = 2 * j + b
+                nc.tensor.matmul_mx(
+                    out=acc[:, b, :],
+                    lhsT=w2_codes[e // EARLY][:, e % EARLY, 2 * P * nb : 2 * P * (nb + 1)].bitcast(FP4X4),
+                    lhsT_scale=w2_planes[:, e, P * nb : P * (nb + 1)],
+                    rhs=codes[:].bitcast(FP8X4),
+                    rhs_scale=scales[:],
+                    start=True,
+                    stop=True,
+                )
+            nc.scalar.copy(out=y_sb[j][:, :, e * C : (e + 1) * C], in_=acc[:])
 
         windows = {}
 
@@ -178,21 +232,42 @@ def tile_moe_pkd_mlp_gelu_kernel(
                 windows[nb][:].indirect(slots_of(e0, e1)), y_sb[nb // 2][:, nb % 2, cols], gate_sb[:, cols], MULT
             )
 
-        second_layer(0, *first_layer(0))
-        load_w1(3, E, "w1_first")
-        gather_words(2, 4, 6, "h_cols0")
+        pair_a, pair_b, pair_c = ("acc0", "acc1"), ("acc2", "acc3"), ("acc4", "acc5")
+        quantized = {}
+
+        quantized[0] = quantize(0, first_layer(0, pair_a, copy_by_half=True))
+        for j in range(2):
+            second_layer(0, j, quantized[0], pair_a[j])
+        gather_words(2, 4, E, "h_cols0")
+        last_planes = keep.tile([P, 2 * PASSES, H], U8, name="last_planes", tag="first_words", align_bytes=64)
+        load_planes(last_planes, 0, w1_scales, 4, E)
+        name_w1_planes(last_planes, 4, E)
         scatter(0, 0, 1, "window0")
-        second_layer(1, *first_layer(1))
-        load_planes(w1s, w1_scales, 4, E, [nc.sync] * 4)
-        second_layer(2, *first_layer(2))
-        scatter(1, 0, 1, "h_cols2")
-        scatter(2, 0, 1, "h_codes2")
+
+        quantized[1] = quantize(1, first_layer(1, pair_b))
+        for j in range(2):
+            second_layer(1, j, quantized[1], pair_b[j])
+        scatter(1, 0, 1, "h_cols1")
+        for nb in range(2):
+            scatter(nb, 1, 2)
+
+        quantized[2] = quantize(2, first_layer(2, pair_a))
+        hidden = {3: first_layer(3, pair_b)}
+        for j in range(2):
+            second_layer(2, j, quantized[2], pair_b[1 - j])
+        scatter(2, 0, 2, "h_cols2")
         for nb in range(3):
-            scatter(nb, 1, 3)
-        hidden = [first_layer(e) for e in range(3, E)]
-        for e in range(3, E):
-            second_layer(e, *hidden[e - 3])
-        scatter(3, 0, 3, "h_cols5")
-        for nb in range(4):
-            scatter(nb, 3, E)
+            scatter(nb, 2, EARLY)
+
+        hidden[4] = first_layer(4, pair_c)
+        hidden[5] = first_layer(5, pair_a, row_tags=("h_codes3", "h_codes4"))
+        for e in range(EARLY, E):
+            quantized[e] = quantize(e, hidden[e])
+        scatter(3, 0, EARLY, "h_cols5")
+        last_banks = ("turned1", pair_a[1])
+        for j in range(2):
+            for e in range(EARLY, E):
+                second_layer(e, j, quantized[e], last_banks[(j * (E - EARLY) + e - EARLY) % 2])
+        for nb in range(BLOCKS):
+            scatter(nb, EARLY, E)
             nc.sync.dma_start(out=out[nb * P : (nb + 1) * P, :], in_=windows[nb][:])

from contextlib import ExitStack

import concourse.mybir as mybir
from concourse.masks import make_identity

K, T, E, C, H, N = 1536, 1536, 6, 256, 512, 512
P = 128
PASSES = K // 512
BLOCKS = N // P
EARLY = E // 2
MARGIN = 64
F32 = mybir.dt.float32
BF16 = mybir.dt.bfloat16
I32 = mybir.dt.int32
U32 = mybir.dt.uint32
U16 = mybir.dt.uint16
U8 = mybir.dt.uint8
FP8X4 = mybir.dt.float8_e4m3fn_x4
FP4X4 = mybir.dt.float4_e2m1fn_x4
GELU = mybir.ActivationFunctionType.Gelu_apprx_tanh
MULT = mybir.AluOpType.mult

FLOPS = 2 * E * C * (K * H + H * N)
WEIGHTS = E * (K * H + H * N)
BYTES = K * T + K * T // 32 + WEIGHTS // 2 + WEIGHTS // 32 + 4 * E * C + 4 * N * T + 2 * P * (E * C // 16)


def tile_moe_pkd_mlp_gelu_kernel(
    tc, x_words, x_scales, w1_words, w1_scales, w2_words, w2_scales, gate, offs, out
):
    nc = tc.nc
    with ExitStack() as ctx:
        keep = ctx.enter_context(tc.tile_pool(name="keep", bufs=1))
        at_scales = ctx.enter_context(tc.tile_pool(name="at_scales", bufs=1))
        at_words = ctx.enter_context(tc.tile_pool(name="at_words", bufs=1))
        ring = ctx.enter_context(tc.tile_pool(name="ring", bufs=3))
        psum = ctx.enter_context(tc.psum_pool(name="psum", bufs=1))

        offsets = keep.tile([P, E * C // 16], U16, name="offsets")
        nc.sync.dma_start(offsets[:], offs)

        def slots_of(e0, e1):
            return offsets[:, e0 * C // 16 : e1 * C // 16]

        early_rows = (EARLY - 1) * PASSES + EARLY
        last_rows = (E - EARLY) * (PASSES + 1)
        last_bytes = last_rows * 2 * H
        early_bytes = early_rows * 2 * H

        xs_tile = at_scales.tile([P, T + 2 * MARGIN], U8, name="xs_tile", align_bytes=64, offset=early_bytes - MARGIN)
        xs_tokens = xs_tile[:, MARGIN : MARGIN + T]
        xs_rows = x_scales.rearrange("a (h c r) t -> c (a h) r t", h=2, c=2).bitcast(I32)
        xs_tokens32 = xs_tokens.bitcast(I32)
        for c in range(2):
            base = 8 + 32 * c
            nc.sync.dma_start(out=xs_tokens32[base : base + 16, :], in_=xs_rows[c, 0:4])
            nc.sync.dma_start(out=xs_tokens32[base + 16 : base + 24, :], in_=xs_rows[c, 4:6])

        xw_tile = at_words.tile([P, T + MARGIN // 2], I32, name="xw_tile", align_bytes=64, offset=last_bytes - MARGIN)
        xw_first = xw_tile[:, MARGIN // 4 : MARGIN // 4 + T]
        nc.sync.dma_start(out=xw_first, in_=x_words[0].rearrange("p t r -> p (t r)").bitcast(I32))

        def load_planes(planes, at, scales, e0, e1):
            n_planes = (e1 - e0) * scales.shape[1]
            rows = scales[e0:e1].rearrange("e s (q r) n -> r q (e s) n", r=4).bitcast(I32)
            for r in range(4):
                nc.sync.dma_start(out=planes[:].bitcast(I32)[r:P:32, at : at + n_planes, :], in_=rows[r])

        w1_codes = {}
        w1_planes = {}

        def load_w1(words, at, e0, e1):
            nc.sync.dma_start(
                out=words[:, at : at + (e1 - e0) * PASSES, :].bitcast(I32),
                in_=w1_words[e0:e1].rearrange("e s p b -> p (e s) b").bitcast(I32),
            )
            for e in range(e0, e1):
                w1_codes[e] = words[:, at + (e - e0) * PASSES : at + (e - e0 + 1) * PASSES, :]

        def name_w1_planes(planes, e0, e1):
            for e in range(e0, e1):
                w1_planes[e] = planes[:, (e - e0) * PASSES : (e - e0 + 1) * PASSES, :]

        first_words = keep.tile([P, PASSES, 2 * H], U8, name="first_words", tag="first_words", align_bytes=64)
        load_w1(first_words, 0, 0, 1)
        first_planes = keep.tile([P, PASSES, H], U8, name="first_planes", align_bytes=64)
        nc.gpsimd.memset(first_planes[:].bitcast(I32), 0)
        load_planes(first_planes, 0, w1_scales, 0, 1)
        name_w1_planes(first_planes, 0, 1)
        xw_rest = keep.tile([P, PASSES - 1, T], I32, name="xw_rest", align_bytes=64)
        nc.sync.dma_start(out=xw_rest[:], in_=x_words[1:PASSES].rearrange("a p t r -> p a (t r)").bitcast(I32))
        for lo, hi in ((0, 8), (32, 40), (64, P)):
            nc.vector.memset(xs_tokens32[lo:hi, :], 0)

        ident = keep.tile([P, P], F32, name="ident")
        make_identity(nc, ident[:])

        xs_slots = keep.tile([P, E * C], U8, name="xs_slots", align_bytes=64)
        for e0, e1 in ((0, EARLY), (EARLY, E)):
            nc.vector.tensor_copy(xs_slots[:, e0 * C : e1 * C], xs_tokens.indirect(slots_of(e0, e1)))

        x_planes = {}

        def move_scale_rows(planes, e0, e1, queue):
            cols = slice(e0 * C // 4, e1 * C // 4)
            for a in range(PASSES):
                for h in range(2):
                    src = 8 + 4 * (2 * a + h)
                    queue.dma_start(
                        out=planes[:].bitcast(I32)[64 * h : 64 * h + 64, a, :],
                        in_=xs_slots[:].bitcast(I32)[src : src + 64, cols],
                    )
            for e in range(e0, e1):
                x_planes[e] = planes[:, :, (e - e0) * C : (e - e0 + 1) * C]

        early_x_planes = keep.tile([P, PASSES, EARLY * C], U8, name="early_x_planes", align_bytes=64)
        move_scale_rows(early_x_planes, 0, EARLY, nc.scalar)
        second_planes = at_scales.tile([P, PASSES, H], U8, name="second_planes", align_bytes=64, offset=early_bytes)
        load_planes(second_planes, 0, w1_scales, 1, 2)
        name_w1_planes(second_planes, 1, 2)

        x_codes = {}

        def gather_words(a, e0, e1, tag):
            window = xw_first if a == 0 else xw_rest[:, a - 1, :]
            words = keep.tile([P, (e1 - e0) * C], U32, name=f"x_codes{a}_{e0}", tag=tag, align_bytes=64)
            nc.vector.tensor_copy(words[:], window.bitcast(U32).indirect(slots_of(e0, e1)))
            for e in range(e0, e1):
                x_codes[a, e] = words[:, (e - e0) * C : (e - e0 + 1) * C]

        gather_words(0, 0, EARLY, "x_codes0_early")
        gather_words(0, EARLY, E, "x_codes0_last")

        early_words = at_scales.tile([P, early_rows, 2 * H], U8, name="early_words", align_bytes=64, offset=0)
        gate_sb = at_scales.tile([P, E * C], F32, name="gate_sb", align_bytes=64, offset=early_bytes + T)
        last_words = at_words.tile([P, last_rows, 2 * H], U8, name="last_words", align_bytes=64, offset=0)
        mid_planes = at_words.tile([P, 2 * PASSES + E, H], U8, name="mid_planes", align_bytes=64, offset=last_bytes)
        last_x_planes = at_words.tile(
            [P, PASSES, (E - EARLY) * C], U8, name="last_x_planes", align_bytes=64, offset=last_bytes + 4 * T
        )
        w2_codes = [early_words[:, (EARLY - 1) * PASSES :, :], last_words[:, (E - EARLY) * PASSES :, :]]
        w2_rows = w2_words.rearrange("e s p b -> p (e s) b").bitcast(I32)
        load_w1(early_words, 0, 1, 2)
        nc.sync.dma_start(out=w2_codes[0].bitcast(I32), in_=w2_rows[:, 0:EARLY, :])
        nc.sync.dma_start(out=gate_sb[:], in_=gate[0:P, :])
        load_w1(early_words, PASSES, 2, EARLY)
        load_planes(mid_planes, 2 * PASSES, w2_scales, 0, E)
        load_planes(mid_planes, 0, w1_scales, 2, 4)
        move_scale_rows(last_x_planes, EARLY, E, nc.sync)
        load_w1(last_words, 0, EARLY, E)
        nc.sync.dma_start(out=w2_codes[1].bitcast(I32), in_=w2_rows[:, EARLY:E, :])
        name_w1_planes(mid_planes, 2, 4)
        w2_planes = mid_planes[:, 2 * PASSES :, :]

        for e in range(EARLY):
            gather_words(1, e, e + 1, f"x_codes1_{e}")
            gather_words(2, e, e + 1, f"x_codes2_{e}")
        gather_words(1, EARLY, E, "x_codes1_last")
        gather_words(2, 3, 4, "x_codes2_3")

        y_sb = [keep.tile([P, 2, E * C], F32, name=f"y_sb{j}") for j in range(BLOCKS // 2)]

        def first_layer(e, banks, row_tags=None, copy_by_half=False):
            turned = psum.tile([P, 2, 2, P], F32, name="turned", tag=f"turned{e % 2}")
            h_cols = keep.tile([P, 4 * C], BF16, name=f"h_cols{e}", tag=f"h_cols{e}", align_bytes=64)
            for half in range(2):
                slots = slice(half * P, (half + 1) * P)
                acc = psum.tile([P, H], F32, name="acc", tag=banks[half])
                for a in range(PASSES):
                    nc.tensor.matmul_mx(
                        out=acc[:],
                        lhsT=x_codes[a, e][:, slots].bitcast(FP8X4),
                        lhsT_scale=x_planes[e][:, a, slots],
                        rhs=w1_codes[e][:, a, :].bitcast(FP4X4),
                        rhs_scale=w1_planes[e][:, a, :],
                        start=(a == 0),
                        stop=(a == PASSES - 1),
                    )
                if row_tags is None:
                    h_rows = ring.tile([P, H], BF16, name="h_rows", align_bytes=64)
                else:
                    h_rows = keep.tile([P, H], BF16, name="h_rows_last", tag=row_tags[half], align_bytes=64)
                nc.scalar.activation(
                    out=h_rows[:].rearrange("s (u p d) -> s u p d", u=2, d=2),
                    in_=acc[:].rearrange("s (p u d) -> s u p d", u=2, d=2),
                    func=GELU,
                )
                pairs = h_rows[:].bitcast(F32)
                for u in range(2):
                    nc.tensor.transpose(turned[:, half, u, :], pairs[:, u * P : (u + 1) * P], ident[:])
                if copy_by_half:
                    nc.scalar.copy(
                        out=h_cols[:].bitcast(F32)[:, half * C : (half + 1) * C].rearrange("p (s u) -> p s u", u=2),
                        in_=turned[:, half].rearrange("p u s -> p s u"),
                    )
            if not copy_by_half:
                nc.scalar.copy(
                    out=h_cols[:].bitcast(F32).rearrange("p (h s u) -> p h s u", h=2, u=2),
                    in_=turned[:].rearrange("p h u s -> p h s u"),
                )
            return h_cols

        def quantize(e, h_cols):
            codes = keep.tile([P, C], U32, name=f"h_codes{e}", tag=f"h_codes{e}", align_bytes=64)
            scales = keep.tile([P, C], U8, name=f"h_scales{e}", align_bytes=64)
            nc.vector.quantize_mx(out=codes[:].bitcast(FP8X4), scales=scales[:], in_=h_cols[:])
            return codes, scales

        def second_layer(e, j, quantized, bank):
            codes, scales = quantized
            acc = psum.tile([P, 2, C], F32, name="y_acc", tag=bank)
            for b in range(2):
                nb = 2 * j + b
                nc.tensor.matmul_mx(
                    out=acc[:, b, :],
                    lhsT=w2_codes[e // EARLY][:, e % EARLY, 2 * P * nb : 2 * P * (nb + 1)].bitcast(FP4X4),
                    lhsT_scale=w2_planes[:, e, P * nb : P * (nb + 1)],
                    rhs=codes[:].bitcast(FP8X4),
                    rhs_scale=scales[:],
                    start=True,
                    stop=True,
                )
            nc.scalar.copy(out=y_sb[j][:, :, e * C : (e + 1) * C], in_=acc[:])

        windows = {}

        def scatter(nb, e0, e1, tag=None):
            if nb not in windows:
                windows[nb] = keep.tile([P, T], F32, name=f"window{nb}", tag=tag, align_bytes=64)
            cols = slice(e0 * C, e1 * C)
            nc.vector.tensor_tensor(
                windows[nb][:].indirect(slots_of(e0, e1)), y_sb[nb // 2][:, nb % 2, cols], gate_sb[:, cols], MULT
            )

        pair_a, pair_b, pair_c = ("acc0", "acc1"), ("acc2", "acc3"), ("acc4", "acc5")
        quantized = {}

        quantized[0] = quantize(0, first_layer(0, pair_a, copy_by_half=True))
        for j in range(2):
            second_layer(0, j, quantized[0], pair_a[j])
        gather_words(2, 4, E, "h_cols0")
        last_planes = keep.tile([P, 2 * PASSES, H], U8, name="last_planes", tag="first_words", align_bytes=64)
        load_planes(last_planes, 0, w1_scales, 4, E)
        name_w1_planes(last_planes, 4, E)
        scatter(0, 0, 1, "window0")

        quantized[1] = quantize(1, first_layer(1, pair_b))
        for j in range(2):
            second_layer(1, j, quantized[1], pair_b[j])
        scatter(1, 0, 1, "h_cols1")
        for nb in range(2):
            scatter(nb, 1, 2)

        quantized[2] = quantize(2, first_layer(2, pair_a))
        hidden = {3: first_layer(3, pair_b)}
        for j in range(2):
            second_layer(2, j, quantized[2], pair_b[1 - j])
        scatter(2, 0, 2, "h_cols2")
        for nb in range(3):
            scatter(nb, 2, EARLY)

        hidden[4] = first_layer(4, pair_c)
        hidden[5] = first_layer(5, pair_a, row_tags=("h_codes3", "h_codes4"))
        for e in range(EARLY, E):
            quantized[e] = quantize(e, hidden[e])
        scatter(3, 0, EARLY, "h_cols5")
        last_banks = ("turned1", pair_a[1])
        for j in range(2):
            for e in range(EARLY, E):
                second_layer(e, j, quantized[e], last_banks[(j * (E - EARLY) + e - EARLY) % 2])
        for nb in range(BLOCKS):
            scatter(nb, EARLY, E)
            nc.sync.dma_start(out=out[nb * P : (nb + 1) * P, :], in_=windows[nb][:])
